import numpy as np, ml_dtypes
CORES = [10,34,74,98]
N = 4
import mx_ref
BF = ml_dtypes.bfloat16
def cols(t, e):
    v = np.concatenate([t.reshape(128, -1, 4), np.zeros((128, 1, 4), BF)], axis=1)
    return np.ascontiguousarray(v[:, e]).reshape(128, -1)
def cut(t, i, w=512):
    return t[:, w * i:w * i + w]
def f(rng, *shape):
    return mx_ref.flush((rng.standard_normal(shape, dtype=np.float32) * np.exp2(rng.integers(-2, 3, shape[:-1] + (1,)))).astype(BF))
def wide(rng, *shape, cols=0):
    v = rng.standard_normal(shape, dtype=np.float32) * np.exp2(rng.integers(-12, 13, shape)).astype(np.float32)
    if cols: v *= np.repeat(np.exp2(rng.integers(-cols, cols + 1, shape[:-2] + (1, shape[-1] // 4))) * (rng.random(shape[:-2] + (1, shape[-1] // 4)) > 0.0625), 4, axis=-1).astype(np.float32)
    return mx_ref.flush(v.astype(BF))
T, CAPP = 640, 48
def normal(rng, *shape):
    return mx_ref.flush(rng.standard_normal(shape, dtype=np.float32).astype(BF))
def once(rng, case):
    g = wide if case == "spread" else normal
    c = g(rng, N, 128, 4 * T).transpose(1, 0, 2).reshape(128, N * T, 4)
    v = (wide if case == "spread" else f)(rng, N, 128, 4 * T)
    if case in ("near", "ties"):
        e = np.stack([q * T + rng.permutation(T) for q in range(N)])
        m = T // 16; s = int(rng.integers(1, N))
        sets = [(e[:, :2 * m], np.roll(e[:, 2 * m:4 * m], -s, axis=0)),
                (e[:, 4 * m:7 * m], e[:, 7 * m:10 * m]),
                (e[:, 10 * m:11 * m], e[:, 11 * m:12 * m], e[:, 12 * m:13 * m]),
                (e[:, 13 * m:14 * m], e[:, 14 * m:15 * m], np.roll(e[:, 15 * m:], -s, axis=0))]
        first, at, place = np.zeros(N * T, int), np.zeros(N * T, int), rng.integers(0, 512, N * T)
        for l in sets:
            l = np.sort(np.stack(l), axis=0)
            for i in range(len(l)):
                first[l[i]] = l[0]; at[l[i]] = i; place[l[i]] = place[l[0]]
        c = c[:, first]
        if case == "near": c[place // 4, np.arange(N * T), place % 4] = (1 + 0.25 * at).astype(BF)
    if case == "negative":
        z = normal(rng, 128, 1, 4).astype(np.float32) * np.float32(2.0 ** 20)
        c = mx_ref.flush((c.astype(np.float32) * np.float32(2.0 ** 20) + z).astype(BF))
    an, fb = [], []
    for r in range(N):
        if case == "ties":
            n = rng.permutation([CAPP, CAPP, 128 - 2 * CAPP, 0]); to = []
            for q in range(N):
                w = rng.choice(q * T + np.flatnonzero(at[q * T:q * T + T] < 2), n[q])
                w[:12] = w[:1]; to += list(w)
            to = np.array(to)
        else:
            n = 24 + rng.multinomial(32, np.full(N, np.divide(1, N)))
            while n.max() > 40: n = 24 + rng.multinomial(32, np.full(N, np.divide(1, N)))
            to = np.repeat(np.arange(N) * T, n) + rng.integers(0, T, 128)
        to = rng.permutation(to)
        other = (to + rng.integers(1, N * T, 128)) % (N * T)
        away = (to + rng.integers(1, N * T, 128)) % (N * T)
        h = rng.permutation(128) < (128 if case == "forbid" else 64 if case in ("plain", "spread") else 0)
        best, second = np.where(h, other, to), np.where(h, to, other)
        ban = np.where(h, other, away)
        if case == "ties": ban = np.where(at[to] > 0, first[to], away)
        t = c[:, best].astype(np.float32) + np.float32(0.5) * c[:, second].astype(np.float32)
        if case == "negative": t = t - np.float32(4.5) * z
        if case == "near":
            t[place[to] // 4, np.arange(128), place[to] % 4] = np.where(at[to] > 0, 1, -1) * np.exp2(-rng.integers(1, 6, 128))
        an.append(mx_ref.flush(t.astype(BF)).reshape(128, 512)); fb.append(ban.astype(np.int32).reshape(128, 1))
    k = np.ascontiguousarray(c.reshape(128, N, 4 * T).transpose(1, 0, 2))
    return {"an": np.stack(an), "k": k, "v": v, "u": f(rng, N, 128, 512), "fb": np.stack(fb)}
def planted(d, case):
    if case not in ("near", "negative", "ties"): return True
    s = scores(d["an"], d["k"])
    if case == "negative": return bool((s < 0).all())
    s = allowed(s, d["fb"])
    if case == "near":
        top = np.partition(s, N * T - 2, axis=1)[:, -2:]
        gap = top[:, 1] - top[:, 0]
        return bool(((gap > 0) & (gap < 2.0 ** -9 * np.abs(top[:, 1]))).sum(axis=1).min() >= 20)
    w = np.argmax(s, axis=1)
    per = (s == s.max(axis=1, keepdims=True)).reshape(N, N, T, 128).sum(axis=2)
    within = np.take_along_axis(per, (w // T)[:, None], axis=1)[:, 0] > 1
    across = (per > 0).sum(axis=1) > 1
    return bool(within.sum(axis=1).min() >= 10 and across.sum() >= 20)
def draw(rng, case):
    for _ in range(50):
        d = once(rng, case)
        if not check_inputs(d) and planted(d, case): return d
    raise RuntimeError("no draw in 50 tries: " + case)
def setup_inputs(rng):
    return draw(rng, "plain")
def setup_inputs_forbid(rng):
    return draw(rng, "forbid")
def setup_inputs_near(rng):
    return draw(rng, "near")
def setup_inputs_negative(rng):
    return draw(rng, "negative")
def setup_inputs_spread(rng):
    return draw(rng, "spread")
def setup_inputs_ties(rng):
    return draw(rng, "ties")
def scores(an, k):
    kq = [mx_ref.quantize(cut(k[q], j)) for q in range(N) for j in range(T // 128)]
    out = []
    for r in range(N):
        a = mx_ref.quantize(an[r])
        out.append(np.concatenate([mx_ref.matmul(b, a) for b in kq]))
    return np.stack(out)
def allowed(s, fb):
    for r in range(N): s[r][fb[r][:, 0], np.arange(128)] = -np.inf
    return s
def winners(an, k, fb):
    return np.argmax(allowed(scores(an, k), fb), axis=1)
def check_inputs(d):
    if d["fb"].min() < 0 or d["fb"].max() >= N * T: return ["fb"]
    b = []; w = winners(d["an"], d["k"], d["fb"])
    for r in range(N):
        if np.bincount(w[r] // T, minlength=N).max() > CAPP: b.append("winners")
    return b
def reference(an, k, v, u, fb):
    w = winners(an, k, fb)
    allv = np.concatenate([v[q] for q in range(N)], axis=1)
    y = np.zeros((N, 128, 128), np.float32)
    for r in range(N):
        y[r] = mx_ref.matmul(mx_ref.quantize(u[r]), mx_ref.quantize(cols(allv, w[r])))
    return {"y": y, "win": w.astype(np.float32).reshape(N, 128, 1)}

@@ -1,0 +1,311 @@
+from concourse.bass import DstId, RemoteDMATransfer
+from concourse.mybir import dt, AluOpType, AxisListType, ActivationFunctionType as AF
+
+N, TK, HALF = 4, 640, 320
+BIG = 1e29
+
+SCRATCH = {
+    "anb": ("sbuf", [128, 512], "bfloat16"), "kb": ("sbuf", [128, 4 * TK], "bfloat16"),
+    "vb": ("sbuf", [128, 4 * TK], "bfloat16"), "ub": ("sbuf", [128, 512], "bfloat16"),
+    "aq": ("sbuf", [128, 128 * N], "float8_e4m3fn_x4"), "asc": ("sbuf", [128, 128 * N], "uint8"),
+    "kq": ("sbuf", [128, TK], "float8_e4m3fn_x4"), "ksc": ("sbuf", [128, TK], "uint8"),
+    "uq": ("sbuf", [128, 128], "float8_e4m3fn_x4"), "usc": ("sbuf", [128, 128], "uint8"),
+    "zq": ("sbuf", [128, 128 * N], "float8_e4m3fn_x4"), "zsc": ("sbuf", [128, 128 * N], "uint8"),
+    "fbi": ("sbuf", [128, 1], "int32"), "fbf": ("sbuf", [128, 1], "float32"), "fbl": ("sbuf", [128, N], "float32"),
+    "it": ("sbuf", [128, TK], "int32"), "iu": ("sbuf", [128, TK], "uint16"),
+    "im": ("sbuf", [128, 32], "int32"), "im2": ("sbuf", [128, 32], "int32"), "mask": ("sbuf", [128, 32], "float32"),
+    "reset": ("sbuf", [32, 128], "float32"), "pc": ("sbuf", [128, 1], "float32"), "pc4": ("sbuf", [128, 1], "float32"),
+    "i4": ("sbuf", [128, N], "float32"),
+    "land": ("sbuf", [128, 2 * N], "float32"), "rm": ("sbuf", [128, N], "float32"), "rj": ("sbuf", [128, N], "float32"),
+    "qs": ("sbuf", [128, 1], "float32"), "val": ("sbuf", [128, 1], "float32"), "oh": ("sbuf", [128, N], "float32"),
+    "ohn": ("sbuf", [128, N], "float32"), "nr": ("sbuf", [128, 1], "float32"), "wn": ("sbuf", [128, 1], "float32"),
+    "yc": ("sbuf", [128, 128 * N], "float32"), "yo": ("sbuf", [128, 128], "float32"),
+    "pa": ("psum", [128, 1024], "float32"), "pb": ("psum", [128, 1024], "float32"), "yp": ("psum", [128, 2048], "float32"),
+}
+for _q in range(N):
+    SCRATCH["pen%d" % _q] = ("sbuf", [128, TK], "bfloat16")
+    SCRATCH["sp%d" % _q] = ("sbuf", [128, TK], "float32")
+    SCRATCH["m%d" % _q] = ("sbuf", [128, TK + 2], "float32")
+    SCRATCH["j%d" % _q] = ("sbuf", [128, TK], "bfloat16")
+    SCRATCH["h%d" % _q] = ("sbuf", [128, 512], "bfloat16")
+    SCRATCH["oq%d" % _q] = ("sbuf", [128, 128], "float8_e4m3fn_x4")
+    SCRATCH["osc%d" % _q] = ("sbuf", [128, 128], "uint8")
+for _q in range(N + 1):
+    SCRATCH["e%d" % _q] = ("sbuf", [32, 128], "float32")
+    SCRATCH["et%d" % _q] = ("sbuf", [32, 128], "float32")
+    SCRATCH["ec%d" % _q] = ("sbuf", [32, 128], "float32")
+    SCRATCH["d%d" % _q] = ("sbuf", [128, 8], "uint16")
+
+SEMAPHORES = (["x%d" % i for i in range(132)] + ["loc", "vgo"] + ["fb%d" % i for i in range(N)]
+              + ["ac%d" % i for i in range(N)] + ["sc%d" % i for i in range(N)] + ["zc%d" % i for i in range(N)])
+
+
+def rank_program(g, core, T, topo):
+    me = T.rank_of(core)
+    if me is None:
+        return
+    V, S, P, Y = g.vector, g.scalar, g.tensor, g.sync
+    queues = {"g": g, "V": V, "S": S, "P": P, "Y": Y}
+    made, seen, need_loc = [], {}, [0]
+
+    def ev(*insts, n=1):
+        name = "x%d" % len(made)
+        made.append((name, n * len(insts)))
+        for inst in insts:
+            inst.then_inc(T.sem[name], n)
+        return made[-1]
+
+    def wait(qn, *evs):
+        for name, n in evs:
+            if (qn, name) not in seen:
+                seen[(qn, name)] = n
+                queues[qn].wait_ge(T.sem[name], n)
+
+    chip = [topo.chip(c) for c in T.cores]
+    near = [q for q in range(N) if q != me and topo.same_plane(chip[q], chip[me])]
+    far = [q for q in range(N) if q != me and q not in near]
+    far.sort(key=lambda q: (q - me) * (1 if me % 2 == 0 else -1) % N)
+    others = near + far
+
+    def where(q):
+        a = topo.addr(T.cores[q])
+        return a[0], a[1], topo.mask(core, T.cores[q]), len(topo.engines(core, T.cores[q]))
+
+    def count(q):
+        return len(topo.engines(T.cores[q], core))
+
+    def send(q, out, in_, sem):
+        rid, pid, mask, n = where(q)
+        g.remote_dma(out, in_, T.sem[sem], T.sem.loc, pid, rid, mask)
+        need_loc[0] += n
+
+    def send_all(out, in_, sem):
+        w = [where(q) for q in others]
+        g.remote_dma_fused([RemoteDMATransfer(dst_ids=[DstId(rid=x[0], pnc=x[1]) for x in w], dma_engine_mask=w[0][2],
+                                              remote_sem=T.sem[sem], srcs=[in_], dsts=[out for _ in w])], local_sem=T.sem.loc)
+        need_loc[0] += w[0][3]
+
+    u8 = dt.uint8
+    A = AluOpType
+
+    def slot(t, q):
+        return T[t][:, 128 * q:128 * q + 128]
+
+    e_an = ev(Y.dma_start(T.anb[:], T.an[:]), n=16)
+    e_fb = ev(S.dma_start(T.fbi[:], T.fb[:]), n=16)
+    e_k = [ev(Y.dma_start(T.kb[:, :4 * HALF], T.k[:, :4 * HALF]), n=16),
+           ev(S.dma_start(T.kb[:, 4 * HALF:], T.k[:, 4 * HALF:]), n=16)]
+    Y.wait_ge(T.sem.vgo, 1)
+    e_v = ev(Y.dma_start(T.vb[:], T.v[:]), n=16)
+    e_u = ev(Y.dma_start(T.ub[:], T.u[:]), n=16)
+
+    e_it = ev(g.iota(T.it[:], [[1, TK]], me * TK, 0))
+    wait("V", e_fb)
+    e_fbf = ev(V.tensor_copy(T.fbf[:], T.fbi[:]))
+    wait("g", e_fbf)
+    send_all(T.fbl[:, me:me + 1], T.fbf[:], "fb%d" % me)
+    wait("V", e_an)
+    e_aq = ev(V.quantize_mx(slot("aq", me), slot("asc", me), T.anb[:]))
+    wait("g", e_aq)
+    send(others[0], slot("aq", me).bitcast(u8), slot("aq", me).bitcast(u8), "ac%d" % me)
+    send_all(slot("asc", me), slot("asc", me), "ac%d" % me)
+    for q in others[1:]:
+        send(q, slot("aq", me).bitcast(u8), slot("aq", me).bitcast(u8), "ac%d" % me)
+    g.sem_inc(T.sem.vgo, 1)
+    e_im = ev(g.iota(T.im[:], [[-1, 32]], 128, 1))
+    e_pc = ev(g.iota(T.pc[:], [[1, 1]], 0, 1, allow_small_or_imprecise_dtypes=True))
+    e_i4 = ev(g.iota(T.i4[:], [[1, N]], 0, 0, allow_small_or_imprecise_dtypes=True))
+
+    wait("V", e_it)
+    e_iu = ev(V.tensor_copy(T.iu[:], T.it[:]))
+    e_kq = []
+    for i in (0, 1):
+        wait("V", e_k[i])
+        c = slice(HALF * i, HALF * i + HALF)
+        e_kq.append(ev(V.quantize_mx(T.kq[:, c], T.ksc[:, c], T.kb[:, 4 * HALF * i:4 * HALF * (i + 1)])))
+
+    order = [me] + others
+    bank = {q: T["pb" if i % 2 else "pa"] for i, q in enumerate(order)}
+    e_pen, e_mm, e_v1, e_m, e_idx, e_e, e_d, e_z = {}, {}, {}, {}, {}, {}, {}, {}
+    e_h = {q: [] for q in range(N)}
+
+    def products(i):
+        q = order[i]
+        if q == me:
+            wait("P", e_aq)
+        else:
+            P.wait_ge(T.sem["ac%d" % q], 2 * count(q))
+        if i >= 2:
+            wait("P", e_v1[order[i - 2]])
+        e_mm[q] = []
+        for b in (0, 1):
+            wait("P", e_kq[b])
+            c = slice(HALF * b, HALF * b + HALF)
+            e_mm[q].append(ev(P.matmul_mx(bank[q][:, 512 * b:512 * b + HALF], slot("aq", q), slot("asc", q),
+                                          T.kq[:, c], T.ksc[:, c], True, True)))
+
+    def penalty(q):
+        if q == me:
+            wait("V", e_fbf)
+            f = T.fbf[:]
+        else:
+            V.wait_ge(T.sem["fb%d" % q], count(q))
+            f = T.fbl[:, q:q + 1]
+        wait("V", e_iu)
+        e_pen[q] = ev(V.tensor_scalar(T["pen%d" % q][:], T.iu[:], f, -BIG, A.is_equal, A.mult))
+
+    def best(q):
+        wait("V", e_pen[q])
+        sp, m, calls = T["sp%d" % q], T["m%d" % q], []
+        for b in (0, 1):
+            wait("V", e_mm[q][b])
+            c = slice(HALF * b, HALF * b + HALF)
+            calls.append(V.tensor_tensor(sp[:, c], bank[q][:, 512 * b:512 * b + HALF], T["pen%d" % q][:, c], A.add))
+        e_v1[q] = ev(*calls)
+        wait("V", e_v1[q])
+        e_m[q] = ev(V.tensor_tensor_scan(m[:, :TK], sp[:], sp[:], -9e29, A.max, A.max))
+
+    def first(q):
+        m = T["m%d" % q]
+        wait("S", e_m[q])
+        e_idx[q] = ev(S.activation(T["j%d" % q][:], m[:, :TK], AF.Sign, bias=m[:, TK - 1:TK], scale=-1.0,
+                                   accum_out=m[:, TK:TK + 1]))
+
+    def spread(n, col, e_col):
+        wait("S", e_col, e_mask)
+        e_e[n] = ev(*[S.activation(T["e%d" % n][:, 32 * a:32 * a + 32], T.mask[32 * a:32 * a + 32, :], AF.Copy,
+                                   scale=col[32 * a:32 * a + 32, :]) for a in range(4)])
+
+    def listed(n):
+        wait("V", e_e[n])
+        wait("V", ev(V.transpose(T["et%d" % n][:], T["e%d" % n][:])))
+        wait("V", e_reset)
+        wait("V", ev(V.tensor_tensor_scan(T["ec%d" % n][:], T.reset[:], T["et%d" % n][:], 0.0, A.mult, A.add)))
+        d, s = T["d%d" % n], T["ec%d" % n][:, 15:128:16]
+        a = ev(V.tensor_copy(d[0:32, :], s), V.tensor_copy(d[32:64, :], s))
+        wait("V", a)
+        e_d[n] = [a, ev(V.tensor_copy(d[64:128, :], d[0:64, :]))]
+
+    def gather(qn, q, ts):
+        wait(qn, e_v, *e_d[q])
+        calls = []
+        for t in ts:
+            win, out = T.vb[:, t:4 * TK].indirect(T["d%d" % q][:, :]), T["h%d" % q][:, t:512:4]
+            calls.append(V.tensor_copy(out, win) if qn == "V" else S.activation(out, win, AF.Copy))
+        e_h[q].append(ev(*calls))
+
+    def pack(q):
+        wait("V", *e_h[q])
+        o, s = (slot("zq", q), slot("zsc", q)) if q == me else (T["oq%d" % q][:], T["osc%d" % q][:])
+        e_z[q] = ev(V.quantize_mx(o, s, T["h%d" % q][:]))
+
+    def send_best(q):
+        wait("g", e_idx[q], e_m[q])
+        send(q, T.land[:, 2 * me:2 * me + 2], T["m%d" % q][:, TK - 1:TK + 1], "sc%d" % me)
+
+    def send_values(q):
+        wait("g", e_z[q])
+        send(q, slot("zq", me).bitcast(u8), T["oq%d" % q][:].bitcast(u8), "zc%d" % me)
+        send(q, slot("zsc", me), T["osc%d" % q][:], "zc%d" % me)
+
+    def score(q):
+        best(q)
+        first(q)
+
+    def index(q):
+        spread(q, T["m%d" % q][:, TK:TK + 1], e_idx[q])
+
+    r1, r2, r3 = others
+    penalty(me)
+    products(0)
+    score(me)
+    products(1)
+    products(2)
+    wait("Y", e_idx[me], e_m[me])
+    e_own = ev(Y.dma_start(T.land[:, 2 * me:2 * me + 2], T["m%d" % me][:, TK - 1:TK + 1]), n=16)
+    wait("V", e_im)
+    wait("V", ev(V.tensor_scalar(T.im2[:], T.im[:], 15, None, A.bitwise_and)))
+    e_mask = ev(V.tensor_scalar(T.mask[:], T.im2[:], 0.0, 4.0, A.is_equal, A.mult))
+    wait("V", ev(V.memset(T.reset[:], 1.0)))
+    e_reset = ev(V.memset(T.reset[:, 0:128:16], 0.0))
+    wait("V", e_pc)
+    e_pc4 = ev(V.tensor_scalar(T.pc4[:], T.pc[:], 0.25, None, A.mult))
+    for q in others:
+        penalty(q)
+
+    score(r1)
+    index(r1)
+    send_best(r1)
+    score(r2)
+    index(r2)
+    send_best(r2)
+    products(3)
+    listed(r1)
+    gather("S", r1, (0, 1, 2, 3))
+    score(r3)
+    index(r3)
+    pack(r1)
+    send_values(r1)
+    send_best(r3)
+    listed(r2)
+    gather("V", r2, (0, 1))
+    gather("S", r2, (2, 3))
+    listed(r3)
+    pack(r2)
+    send_values(r2)
+    gather("V", r3, (0, 1))
+    gather("S", r3, (2, 3))
+    pack(r3)
+    send_values(r3)
+
+    index(me)
+    listed(me)
+    gather("V", me, (0, 1))
+    gather("S", me, (2, 3))
+    wait("V", e_u)
+    e_uq = ev(V.quantize_mx(T.uq[:], T.usc[:], T.ub[:]))
+    pack(me)
+    wait("P", e_uq)
+    e_y = {}
+    for q in order:
+        if q == me:
+            wait("P", e_z[me])
+        else:
+            P.wait_ge(T.sem["zc%d" % q], 2 * count(q))
+        e_y[q] = ev(P.matmul_mx(T.yp[:, 512 * q:512 * q + 128], T.uq[:], T.usc[:], slot("zq", q), slot("zsc", q), True, True))
+
+    for q in others:
+        V.wait_ge(T.sem["sc%d" % q], count(q))
+    wait("V", e_own)
+    best_s = T.land[:, 0:2 * N:2]
+    e_rm = ev(V.tensor_tensor_scan(T.rm[:], best_s, best_s, -9e29, A.max, A.max))
+    wait("S", e_rm)
+    e_qs = ev(S.activation(T.rj[:], T.rm[:], AF.Sign, bias=T.rm[:, N - 1:N], scale=-1.0, accum_out=T.qs[:]))
+    wait("V", e_qs, e_pc4)
+    e_val = ev(V.tensor_scalar(T.val[:], T.qs[:], 32.0, T.pc4[:], A.mult, A.add))
+    spread(N, T.val, e_val)
+    wait("V", e_i4)
+    wait("V", ev(V.tensor_scalar(T.oh[:], T.i4[:], T.qs[:], None, A.is_equal)))
+    wait("V", ev(V.tensor_tensor(T.ohn[:], T.oh[:], T.land[:, 1:2 * N:2], A.mult)))
+    wait("V", ev(V.tensor_reduce(T.nr[:], T.ohn[:], AxisListType.X, A.add)))
+    e_wn = ev(V.tensor_scalar(T.wn[:], T.qs[:], float(TK), T.nr[:], A.mult, A.add))
+    wait("Y", e_wn)
+    e_w = ev(Y.dma_start(T.win[:], T.wn[:]), n=16)
+    listed(N)
+
+    calls = []
+    for q in order:
+        wait("V", e_y[q])
+        calls.append(V.tensor_copy(slot("yc", q), T.yp[:, 512 * q:512 * q + 128]))
+    wait("V", ev(*calls))
+    wait("V", *e_d[N])
+    e_yo = ev(V.tensor_copy(T.yo[:], T.yc[:].indirect(T["d%d" % N][:, :])))
+    wait("Y", e_yo)
+    e_out = ev(Y.dma_start(T.y[:], T.yo[:]), n=16)
+    wait("Y", e_w, e_out)
+
+    g.wait_ge(T.sem.loc, need_loc[0])
+    waited = set(name for _, name in seen)
+    for name, n in made:
+        if name not in waited:
+            g.wait_ge(T.sem[name], n)

@@ -12,7 +12,7 @@ SCRATCH = {
     "uq": ("sbuf", [128, 128], "float8_e4m3fn_x4"), "usc": ("sbuf", [128, 128], "uint8"),
     "zq": ("sbuf", [128, 128 * N], "float8_e4m3fn_x4"), "zsc": ("sbuf", [128, 128 * N], "uint8"),
     "fbi": ("sbuf", [128, 1], "int32"), "fbf": ("sbuf", [128, 1], "float32"), "fbl": ("sbuf", [128, N], "float32"),
-    "it": ("sbuf", [128, TK], "int32"), "iu": ("sbuf", [128, TK], "uint16"),
+    "it": ("sbuf", [128, HALF], "int32"), "iu": ("sbuf", [128, TK], "uint16"),
     "im": ("sbuf", [128, 32], "int32"), "im2": ("sbuf", [128, 32], "int32"), "mask": ("sbuf", [128, 32], "float32"),
     "reset": ("sbuf", [32, 128], "float32"), "pc": ("sbuf", [128, 1], "float32"), "pc4": ("sbuf", [128, 1], "float32"),
     "i4": ("sbuf", [128, N], "float32"),
@@ -61,29 +61,40 @@ def rank_program(g, core, T, topo):
                 seen[(qn, name)] = n
                 queues[qn].wait_ge(T.sem[name], n)
 
-    chip = [topo.chip(c) for c in T.cores]
-    near = [q for q in range(N) if q != me and topo.same_plane(chip[q], chip[me])]
-    far = [q for q in range(N) if q != me and q not in near]
-    far.sort(key=lambda q: (q - me) * (1 if me % 2 == 0 else -1) % N)
-    others = near + far
+    def others_of(r):
+        chip = [topo.chip(c) for c in T.cores]
+        near = [q for q in range(N) if q != r and topo.same_plane(chip[q], chip[r])]
+        far = [q for q in range(N) if q != r and q not in near]
+        far.sort(key=lambda q: (q - r) * (1 if r % 2 == 0 else -1) % N)
+        return near + far
 
-    def where(q):
+    others = others_of(me)
+
+    def split(src, q, parts):
+        e = topo.engines(src, T.cores[q])
+        if parts:
+            i, n = parts
+            w = 1
+            while 2 * w * n <= len(e):
+                w *= 2
+            e = e[w * i:w * i + w]
+        return e
+
+    def addr(q):
         a = topo.addr(T.cores[q])
-        return a[0], a[1], topo.mask(core, T.cores[q]), len(topo.engines(core, T.cores[q]))
+        return DstId(rid=a[0], pnc=a[1])
 
-    def count(q):
-        return len(topo.engines(T.cores[q], core))
+    def send(moves, sem):
+        ts = []
+        for i, (qs, out, in_) in enumerate(moves):
+            e = split(core, qs[0], (i, len(moves)) if len(moves) > 1 else None)
+            need_loc[0] += len(e)
+            ts.append(RemoteDMATransfer(dst_ids=[addr(q) for q in qs], dma_engine_mask=sum(1 << x for x in e),
+                                        remote_sem=T.sem[sem], srcs=[in_], dsts=[out for _ in qs]))
+        g.remote_dma_fused(ts, local_sem=T.sem.loc)
 
-    def send(q, out, in_, sem):
-        rid, pid, mask, n = where(q)
-        g.remote_dma(out, in_, T.sem[sem], T.sem.loc, pid, rid, mask)
-        need_loc[0] += n
-
-    def send_all(out, in_, sem):
-        w = [where(q) for q in others]
-        g.remote_dma_fused([RemoteDMATransfer(dst_ids=[DstId(rid=x[0], pnc=x[1]) for x in w], dma_engine_mask=w[0][2],
-                                              remote_sem=T.sem[sem], srcs=[in_], dsts=[out for _ in w])], local_sem=T.sem.loc)
-        need_loc[0] += w[0][3]
+    def count(q, place=None):
+        return len(split(T.cores[q], me, place))
 
     u8 = dt.uint8
     A = AluOpType
@@ -99,34 +110,35 @@ def rank_program(g, core, T, topo):
     e_v = ev(Y.dma_start(T.vb[:], T.v[:]), n=16)
     e_u = ev(Y.dma_start(T.ub[:], T.u[:]), n=16)
 
-    e_it = ev(g.iota(T.it[:], [[1, TK]], me * TK, 0))
+    e_it = ev(g.iota(T.it[:], [[1, HALF]], me * TK, 0))
+    e_im = ev(g.iota(T.im[:], [[-1, 32]], 128, 1))
+    e_pc = ev(g.iota(T.pc[:], [[1, 1]], 0, 1, allow_small_or_imprecise_dtypes=True))
+    wait("V", ev(V.memset(T.reset[:], 1.0)))
+    e_reset = ev(V.memset(T.reset[:, 0:128:16], 0.0))
+    wait("V", e_it)
+    e_iu = ev(V.tensor_copy(T.iu[:, :HALF], T.it[:]), V.tensor_scalar(T.iu[:, HALF:], T.it[:], float(HALF), None, A.add))
+    wait("V", e_im)
+    wait("V", ev(V.tensor_scalar(T.im2[:], T.im[:], 15, None, A.bitwise_and)))
+    e_mask = ev(V.tensor_scalar(T.mask[:], T.im2[:], 0.0, 4.0, A.is_equal, A.mult))
+    wait("V", e_pc)
+    e_pc4 = ev(V.tensor_scalar(T.pc4[:], T.pc[:], 0.25, None, A.mult))
     wait("V", e_fb)
     e_fbf = ev(V.tensor_copy(T.fbf[:], T.fbi[:]))
     wait("g", e_fbf)
-    send_all(T.fbl[:, me:me + 1], T.fbf[:], "fb%d" % me)
+    send([(others, T.fbl[:, me:me + 1], T.fbf[:])], "fb%d" % me)
     wait("V", e_an)
     e_aq = ev(V.quantize_mx(slot("aq", me), slot("asc", me), T.anb[:]))
     wait("g", e_aq)
-    send(others[0], slot("aq", me).bitcast(u8), slot("aq", me).bitcast(u8), "ac%d" % me)
-    send_all(slot("asc", me), slot("asc", me), "ac%d" % me)
-    for q in others[1:]:
-        send(q, slot("aq", me).bitcast(u8), slot("aq", me).bitcast(u8), "ac%d" % me)
+    mine = slot("aq", me).bitcast(u8)
+    send([(others[:1], mine, mine)], "ac%d" % me)
+    send([(others, slot("asc", me), slot("asc", me))], "ac%d" % me)
+    send([(others[1:], mine, mine)], "ac%d" % me)
     g.sem_inc(T.sem.vgo, 1)
-    e_im = ev(g.iota(T.im[:], [[-1, 32]], 128, 1))
-    e_pc = ev(g.iota(T.pc[:], [[1, 1]], 0, 1, allow_small_or_imprecise_dtypes=True))
     e_i4 = ev(g.iota(T.i4[:], [[1, N]], 0, 0, allow_small_or_imprecise_dtypes=True))
-
-    wait("V", e_it)
-    e_iu = ev(V.tensor_copy(T.iu[:], T.it[:]))
-    e_kq = []
-    for i in (0, 1):
-        wait("V", e_k[i])
-        c = slice(HALF * i, HALF * i + HALF)
-        e_kq.append(ev(V.quantize_mx(T.kq[:, c], T.ksc[:, c], T.kb[:, 4 * HALF * i:4 * HALF * (i + 1)])))
 
     order = [me] + others
     bank = {q: T["pb" if i % 2 else "pa"] for i, q in enumerate(order)}
-    e_pen, e_mm, e_v1, e_m, e_idx, e_e, e_d, e_z = {}, {}, {}, {}, {}, {}, {}, {}
+    e_kq, e_pen, e_mm, e_v1, e_m, e_idx, e_e, e_d, e_z, e_l = [], {}, {}, {}, {}, {}, {}, {}, {}, {}
     e_h = {q: [] for q in range(N)}
 
     def products(i):
@@ -136,13 +148,14 @@ def rank_program(g, core, T, topo):
         else:
             P.wait_ge(T.sem["ac%d" % q], 2 * count(q))
         if i >= 2:
-            wait("P", e_v1[order[i - 2]])
+            wait("P", *e_v1[order[i - 2]])
         e_mm[q] = []
         for b in (0, 1):
             wait("P", e_kq[b])
             c = slice(HALF * b, HALF * b + HALF)
             e_mm[q].append(ev(P.matmul_mx(bank[q][:, 512 * b:512 * b + HALF], slot("aq", q), slot("asc", q),
                                           T.kq[:, c], T.ksc[:, c], True, True)))
+        e_v1[q] = []
 
     def penalty(q):
         if q == me:
@@ -154,39 +167,45 @@ def rank_program(g, core, T, topo):
         wait("V", e_iu)
         e_pen[q] = ev(V.tensor_scalar(T["pen%d" % q][:], T.iu[:], f, -BIG, A.is_equal, A.mult))
 
-    def best(q):
-        wait("V", e_pen[q])
-        sp, m, calls = T["sp%d" % q], T["m%d" % q], []
-        for b in (0, 1):
-            wait("V", e_mm[q][b])
-            c = slice(HALF * b, HALF * b + HALF)
-            calls.append(V.tensor_tensor(sp[:, c], bank[q][:, 512 * b:512 * b + HALF], T["pen%d" % q][:, c], A.add))
-        e_v1[q] = ev(*calls)
-        wait("V", e_v1[q])
-        e_m[q] = ev(V.tensor_tensor_scan(m[:, :TK], sp[:], sp[:], -9e29, A.max, A.max))
+    def forbid(q, b):
+        wait("V", e_pen[q], e_mm[q][b])
+        c = slice(HALF * b, HALF * b + HALF)
+        e_v1[q].append(ev(V.tensor_tensor(T["sp%d" % q][:, c], bank[q][:, 512 * b:512 * b + HALF], T["pen%d" % q][:, c], A.add)))
 
-    def first(q):
-        m = T["m%d" % q]
-        wait("S", e_m[q])
-        e_idx[q] = ev(S.activation(T["j%d" % q][:], m[:, :TK], AF.Sign, bias=m[:, TK - 1:TK], scale=-1.0,
-                                   accum_out=m[:, TK:TK + 1]))
+    def best(q):
+        wait("V", *e_v1[q])
+        e_m[q] = ev(V.tensor_tensor_scan(T["m%d" % q][:, :TK], T["sp%d" % q][:], T["sp%d" % q][:], -9e29, A.max, A.max))
 
     def spread(n, col, e_col):
         wait("S", e_col, e_mask)
         e_e[n] = ev(*[S.activation(T["e%d" % n][:, 32 * a:32 * a + 32], T.mask[32 * a:32 * a + 32, :], AF.Copy,
                                    scale=col[32 * a:32 * a + 32, :]) for a in range(4)])
 
-    def listed(n):
-        wait("V", e_e[n])
-        wait("V", ev(V.transpose(T["et%d" % n][:], T["e%d" % n][:])))
-        wait("V", e_reset)
-        wait("V", ev(V.tensor_tensor_scan(T["ec%d" % n][:], T.reset[:], T["et%d" % n][:], 0.0, A.mult, A.add)))
-        d, s = T["d%d" % n], T["ec%d" % n][:, 15:128:16]
-        a = ev(V.tensor_copy(d[0:32, :], s), V.tensor_copy(d[32:64, :], s))
-        wait("V", a)
-        e_d[n] = [a, ev(V.tensor_copy(d[64:128, :], d[0:64, :]))]
+    def first(q):
+        m = T["m%d" % q]
+        wait("S", e_m[q])
+        e_idx[q] = ev(S.activation(T["j%d" % q][:], m[:, :TK], AF.Sign, bias=m[:, TK - 1:TK], scale=-1.0,
+                                   accum_out=m[:, TK:TK + 1]))
+        spread(q, m[:, TK:TK + 1], e_idx[q])
 
-    def gather(qn, q, ts):
+    def list1(n):
+        wait("V", e_e[n])
+        e_l[n] = ev(V.transpose(T["et%d" % n][:], T["e%d" % n][:]))
+
+    def list2(n):
+        wait("V", e_l[n], e_reset)
+        e_l[n] = ev(V.tensor_tensor_scan(T["ec%d" % n][:], T.reset[:], T["et%d" % n][:], 0.0, A.mult, A.add))
+
+    def list3(n):
+        wait("V", e_l[n])
+        d, s = T["d%d" % n], T["ec%d" % n][:, 15:128:16]
+        e_d[n] = [ev(V.tensor_copy(d[0:32, :], s), V.tensor_copy(d[32:64, :], s))]
+
+    def list4(n):
+        wait("V", *e_d[n])
+        e_d[n].append(ev(V.tensor_copy(T["d%d" % n][64:128, :], T["d%d" % n][0:64, :])))
+
+    def gather(qn, q, *ts):
         wait(qn, e_v, *e_d[q])
         calls = []
         for t in ts:
@@ -199,105 +218,126 @@ def rank_program(g, core, T, topo):
         o, s = (slot("zq", q), slot("zsc", q)) if q == me else (T["oq%d" % q][:], T["osc%d" % q][:])
         e_z[q] = ev(V.quantize_mx(o, s, T["h%d" % q][:]))
 
-    def send_best(q):
-        wait("g", e_idx[q], e_m[q])
-        send(q, T.land[:, 2 * me:2 * me + 2], T["m%d" % q][:, TK - 1:TK + 1], "sc%d" % me)
-
-    def send_values(q):
+    def ship_codes(q):
         wait("g", e_z[q])
-        send(q, slot("zq", me).bitcast(u8), T["oq%d" % q][:].bitcast(u8), "zc%d" % me)
-        send(q, slot("zsc", me), T["osc%d" % q][:], "zc%d" % me)
+        send([([q], slot("zq", me).bitcast(u8), T["oq%d" % q][:].bitcast(u8))], "zc%d" % me)
 
-    def score(q):
-        best(q)
-        first(q)
-
-    def index(q):
-        spread(q, T["m%d" % q][:, TK:TK + 1], e_idx[q])
+    def ship_scales(*qs):
+        send([([q], slot("zsc", me), T["osc%d" % q][:]) for q in qs], "zc%d" % me)
 
     r1, r2, r3 = others
     penalty(me)
+    for i in (0, 1):
+        wait("V", e_k[i])
+        c = slice(HALF * i, HALF * i + HALF)
+        e_kq.append(ev(V.quantize_mx(T.kq[:, c], T.ksc[:, c], T.kb[:, 4 * HALF * i:4 * HALF * (i + 1)])))
     products(0)
-    score(me)
-    products(1)
-    products(2)
+    forbid(me, 0)
+    forbid(me, 1)
+    best(me)
+    first(me)
     wait("Y", e_idx[me], e_m[me])
     e_own = ev(Y.dma_start(T.land[:, 2 * me:2 * me + 2], T["m%d" % me][:, TK - 1:TK + 1]), n=16)
-    wait("V", e_im)
-    wait("V", ev(V.tensor_scalar(T.im2[:], T.im[:], 15, None, A.bitwise_and)))
-    e_mask = ev(V.tensor_scalar(T.mask[:], T.im2[:], 0.0, 4.0, A.is_equal, A.mult))
-    wait("V", ev(V.memset(T.reset[:], 1.0)))
-    e_reset = ev(V.memset(T.reset[:, 0:128:16], 0.0))
-    wait("V", e_pc)
-    e_pc4 = ev(V.tensor_scalar(T.pc4[:], T.pc[:], 0.25, None, A.mult))
     for q in others:
         penalty(q)
 
-    score(r1)
-    index(r1)
-    send_best(r1)
-    score(r2)
-    index(r2)
-    send_best(r2)
+    products(1)
+    forbid(r1, 0)
+    forbid(r1, 1)
+    list1(me)
+    best(r1)
+    first(r1)
+    list2(me)
+    products(2)
+    forbid(r2, 0)
+    list3(me)
+    forbid(r2, 1)
+    list4(me)
+    best(r2)
+    first(r2)
     products(3)
-    listed(r1)
-    gather("S", r1, (0, 1, 2, 3))
-    score(r3)
-    index(r3)
+    forbid(r3, 0)
+    list1(r1)
+    forbid(r3, 1)
+    list2(r1)
+    list3(r1)
+    list4(r1)
+    gather("S", r1, 0, 1, 2, 3)
+    best(r3)
+    first(r3)
+    list1(r2)
+    list2(r2)
+    list3(r2)
     pack(r1)
-    send_values(r1)
-    send_best(r3)
-    listed(r2)
-    gather("V", r2, (0, 1))
-    gather("S", r2, (2, 3))
-    listed(r3)
+    ship_codes(r1)
+    wait("g", *[e_m[q] for q in others] + [e_idx[q] for q in others])
+    send([([q], T.land[:, 2 * me:2 * me + 2], T["m%d" % q][:, TK - 1:TK + 1]) for q in others], "sc%d" % me)
+    list4(r2)
+    gather("V", r2, 0)
+    gather("S", r2, 2, 3)
+    list1(r3)
+    gather("V", r2, 1)
+    list2(r3)
+    list3(r3)
     pack(r2)
-    send_values(r2)
-    gather("V", r3, (0, 1))
-    gather("S", r3, (2, 3))
+    ship_codes(r2)
+    ship_scales(r1, r2)
+    list4(r3)
+    gather("V", r3, 0, 1)
+    gather("S", r3, 2, 3)
     pack(r3)
-    send_values(r3)
+    ship_codes(r3)
+    ship_scales(r3)
 
-    index(me)
-    listed(me)
-    gather("V", me, (0, 1))
-    gather("S", me, (2, 3))
-    wait("V", e_u)
-    e_uq = ev(V.quantize_mx(T.uq[:], T.usc[:], T.ub[:]))
-    pack(me)
-    wait("P", e_uq)
-    e_y = {}
-    for q in order:
-        if q == me:
-            wait("P", e_z[me])
-        else:
-            P.wait_ge(T.sem["zc%d" % q], 2 * count(q))
-        e_y[q] = ev(P.matmul_mx(T.yp[:, 512 * q:512 * q + 128], T.uq[:], T.usc[:], slot("zq", q), slot("zsc", q), True, True))
-
+    gather("V", me, 0, 1)
+    gather("S", me, 2, 3)
     for q in others:
-        V.wait_ge(T.sem["sc%d" % q], count(q))
+        V.wait_ge(T.sem["sc%d" % q], count(q, (others_of(q).index(me), N - 1)))
     wait("V", e_own)
     best_s = T.land[:, 0:2 * N:2]
     e_rm = ev(V.tensor_tensor_scan(T.rm[:], best_s, best_s, -9e29, A.max, A.max))
     wait("S", e_rm)
     e_qs = ev(S.activation(T.rj[:], T.rm[:], AF.Sign, bias=T.rm[:, N - 1:N], scale=-1.0, accum_out=T.qs[:]))
+    pack(me)
+    wait("V", e_u)
+    e_uq = ev(V.quantize_mx(T.uq[:], T.usc[:], T.ub[:]))
     wait("V", e_qs, e_pc4)
     e_val = ev(V.tensor_scalar(T.val[:], T.qs[:], 32.0, T.pc4[:], A.mult, A.add))
     spread(N, T.val, e_val)
     wait("V", e_i4)
-    wait("V", ev(V.tensor_scalar(T.oh[:], T.i4[:], T.qs[:], None, A.is_equal)))
-    wait("V", ev(V.tensor_tensor(T.ohn[:], T.oh[:], T.land[:, 1:2 * N:2], A.mult)))
-    wait("V", ev(V.tensor_reduce(T.nr[:], T.ohn[:], AxisListType.X, A.add)))
+    e_oh = ev(V.tensor_scalar(T.oh[:], T.i4[:], T.qs[:], None, A.is_equal))
+
+    wait("P", e_uq)
+    e_y, copies = {}, []
+    for q in order:
+        if q == me:
+            wait("P", e_z[me])
+        else:
+            i = others_of(q).index(me)
+            P.wait_ge(T.sem["zc%d" % q], count(q) + count(q, (i, 2) if i < 2 else None))
+        e_y[q] = ev(P.matmul_mx(T.yp[:, 512 * q:512 * q + 128], T.uq[:], T.usc[:], slot("zq", q), slot("zsc", q), True, True))
+
+    def fetch(q):
+        wait("V", e_y[q])
+        copies.append(V.tensor_copy(slot("yc", q), T.yp[:, 512 * q:512 * q + 128]))
+
+    fetch(me)
+    list1(N)
+    wait("V", e_oh)
+    e_ohn = ev(V.tensor_tensor(T.ohn[:], T.oh[:], T.land[:, 1:2 * N:2], A.mult))
+    list2(N)
+    wait("V", e_ohn)
+    e_nr = ev(V.tensor_reduce(T.nr[:], T.ohn[:], AxisListType.X, A.add))
+    list3(N)
+    wait("V", e_nr)
     e_wn = ev(V.tensor_scalar(T.wn[:], T.qs[:], float(TK), T.nr[:], A.mult, A.add))
+    list4(N)
     wait("Y", e_wn)
     e_w = ev(Y.dma_start(T.win[:], T.wn[:]), n=16)
-    listed(N)
 
-    calls = []
-    for q in order:
-        wait("V", e_y[q])
-        calls.append(V.tensor_copy(slot("yc", q), T.yp[:, 512 * q:512 * q + 128]))
-    wait("V", ev(*calls))
+    for q in others:
+        fetch(q)
+    wait("V", ev(*copies))
     wait("V", *e_d[N])
     e_yo = ev(V.tensor_copy(T.yo[:], T.yc[:].indirect(T["d%d" % N][:, :])))
     wait("Y", e_yo)

@@ -1,8 +1,9 @@
 from concourse.bass import DstId, RemoteDMATransfer
 from concourse.mybir import dt, AluOpType, AxisListType, ActivationFunctionType as AF
 
-N, TK, HALF = 4, 640, 320
+N, TK, HALF, QUART = 4, 640, 320, 160
 BIG = 1e29
+HELPED = 2
 
 SCRATCH = {
     "anb": ("sbuf", [128, 512], "bfloat16"), "kb": ("sbuf", [128, 4 * TK], "bfloat16"),
@@ -12,7 +13,7 @@ SCRATCH = {
     "uq": ("sbuf", [128, 128], "float8_e4m3fn_x4"), "usc": ("sbuf", [128, 128], "uint8"),
     "zq": ("sbuf", [128, 128 * N], "float8_e4m3fn_x4"), "zsc": ("sbuf", [128, 128 * N], "uint8"),
     "fbi": ("sbuf", [128, 1], "int32"), "fbf": ("sbuf", [128, 1], "float32"), "fbl": ("sbuf", [128, N], "float32"),
-    "it": ("sbuf", [128, HALF], "int32"), "iu": ("sbuf", [128, TK], "uint16"),
+    "it": ("sbuf", [128, QUART], "int32"), "iu": ("sbuf", [128, TK], "uint16"),
     "im": ("sbuf", [128, 32], "int32"), "im2": ("sbuf", [128, 32], "int32"), "mask": ("sbuf", [128, 32], "float32"),
     "reset": ("sbuf", [32, 128], "float32"), "pc": ("sbuf", [128, 1], "float32"), "pc4": ("sbuf", [128, 1], "float32"),
     "i4": ("sbuf", [128, N], "float32"),
@@ -36,17 +37,47 @@ for _q in range(N + 1):
     SCRATCH["ec%d" % _q] = ("sbuf", [32, 128], "float32")
     SCRATCH["d%d" % _q] = ("sbuf", [128, 8], "uint16")
 
-SEMAPHORES = (["x%d" % i for i in range(132)] + ["loc", "vgo"] + ["fb%d" % i for i in range(N)]
-              + ["ac%d" % i for i in range(N)] + ["sc%d" % i for i in range(N)] + ["zc%d" % i for i in range(N)])
+SEMAPHORES = (["x%d" % i for i in range(115)] + ["loc", "lok", "kc0", "kc1", "ks", "dl"]
+              + ["fb%d" % i for i in range(N)] + ["ac%d" % i for i in range(N)] + ["sc%d" % i for i in range(N)]
+              + ["zc%d" % i for i in range(N)])
+
+PLAN = """
+consts; pen m; ksend; vload; mm m; f m 0; f m 1; best m; ix m; spread m; own; consts2; pen a; pen b;
+mm a; f a 0; l1 m; f a 1; l2 m; best a; ix a; spread a; score a; l3 m; mm b; f b 0; l4 m; f b 1; best b; l1 a; ix b;
+spread b; score b; l2 a; l3 a; l4 a; gV a 0 1; gS a 2 3; l1 b; l2 b; l3 b; l4 b; pack a; ship a; gV b 0 1; gS b 2 3;
+pack b; ship b; gV h 0 1; gS h 2 3; pack h; ship h; gV m 0 1; gS m 2 3
+"""
 
 
 def rank_program(g, core, T, topo):
-    me = T.rank_of(core)
-    if me is None:
-        return
     V, S, P, Y = g.vector, g.scalar, g.tensor, g.sync
     queues = {"g": g, "V": V, "S": S, "P": P, "Y": Y}
-    made, seen, need_loc = [], {}, [0]
+    u8 = dt.uint8
+    A = AluOpType
+    chip = [topo.chip(c) for c in T.cores]
+
+    def others_of(r):
+        near = [q for q in range(N) if q != r and topo.same_plane(chip[q], chip[r])]
+        far = [q for q in range(N) if q != r and q not in near]
+        far.sort(key=lambda q: (q - r) * (1 if r % 2 == 0 else -1) % N)
+        return near + far
+
+    def helper_of(r):
+        c0 = T.cores[r]
+        return [c for c in topo.cores_of(c0) if c != c0 and topo.die(c) == topo.die(c0)
+                and all(topo.may_write(c, d) for d in T.cores)][0]
+
+    def site(r, q):
+        return helper_of(r) if q == others_of(r)[HELPED] else T.cores[r]
+
+    owners = [r for r in range(N) if core in (T.cores[r], helper_of(r))]
+    if not owners:
+        return
+    me, = owners
+    others, home = others_of(me), T.cores[me]
+    hlp, hq = helper_of(me), others_of(me)[HELPED]
+    two = [q for q in others if q != hq]
+    made, seen, need = [], {}, {}
 
     def ev(*insts, n=1):
         name = "x%d" % len(made)
@@ -61,139 +92,95 @@ def rank_program(g, core, T, topo):
                 seen[(qn, name)] = n
                 queues[qn].wait_ge(T.sem[name], n)
 
-    def others_of(r):
-        chip = [topo.chip(c) for c in T.cores]
-        near = [q for q in range(N) if q != r and topo.same_plane(chip[q], chip[r])]
-        far = [q for q in range(N) if q != r and q not in near]
-        far.sort(key=lambda q: (q - r) * (1 if r % 2 == 0 else -1) % N)
-        return near + far
+    slow = topo.engines(home, T.cores[others[0]])
+    inner = [e for e in topo.engines(home, hlp) if e not in slow]
+    kmask = [inner, inner + slow]
 
-    others = others_of(me)
+    def count(src):
+        return len(topo.engines(src, core))
 
-    def split(src, q, parts):
-        e = topo.engines(src, T.cores[q])
-        if parts:
-            i, n = parts
-            w = 1
-            while 2 * w * n <= len(e):
-                w *= 2
-            e = e[w * i:w * i + w]
-        return e
-
-    def addr(q):
-        a = topo.addr(T.cores[q])
+    def addr(c):
+        a = topo.addr(c)
         return DstId(rid=a[0], pnc=a[1])
 
-    def send(moves, sem):
-        ts = []
-        for i, (qs, out, in_) in enumerate(moves):
-            e = split(core, qs[0], (i, len(moves)) if len(moves) > 1 else None)
-            need_loc[0] += len(e)
-            ts.append(RemoteDMATransfer(dst_ids=[addr(q) for q in qs], dma_engine_mask=sum(1 << x for x in e),
-                                        remote_sem=T.sem[sem], srcs=[in_], dsts=[out for _ in qs]))
-        g.remote_dma_fused(ts, local_sem=T.sem.loc)
-
-    def count(q, place=None):
-        return len(split(T.cores[q], me, place))
-
-    u8 = dt.uint8
-    A = AluOpType
+    def send(dests, out, in_, sem, eng=None, loc="loc"):
+        e = eng or topo.engines(core, dests[0])
+        need[loc] = need.get(loc, 0) + len(e)
+        g.remote_dma_fused([RemoteDMATransfer(dst_ids=[addr(c) for c in dests], dma_engine_mask=sum(1 << x for x in e),
+                                              remote_sem=T.sem[sem], srcs=[in_], dsts=[out for _ in dests])],
+                           local_sem=T.sem[loc])
 
     def slot(t, q):
         return T[t][:, 128 * q:128 * q + 128]
 
-    e_an = ev(Y.dma_start(T.anb[:], T.an[:]), n=16)
-    e_fb = ev(S.dma_start(T.fbi[:], T.fb[:]), n=16)
-    e_k = [ev(Y.dma_start(T.kb[:, :4 * HALF], T.k[:, :4 * HALF]), n=16),
-           ev(S.dma_start(T.kb[:, 4 * HALF:], T.k[:, 4 * HALF:]), n=16)]
-    Y.wait_ge(T.sem.vgo, 1)
-    e_v = ev(Y.dma_start(T.vb[:], T.v[:]), n=16)
-    e_u = ev(Y.dma_start(T.ub[:], T.u[:]), n=16)
-
-    e_it = ev(g.iota(T.it[:], [[1, HALF]], me * TK, 0))
-    e_im = ev(g.iota(T.im[:], [[-1, 32]], 128, 1))
-    e_pc = ev(g.iota(T.pc[:], [[1, 1]], 0, 1, allow_small_or_imprecise_dtypes=True))
-    wait("V", ev(V.memset(T.reset[:], 1.0)))
-    e_reset = ev(V.memset(T.reset[:, 0:128:16], 0.0))
-    wait("V", e_it)
-    e_iu = ev(V.tensor_copy(T.iu[:, :HALF], T.it[:]), V.tensor_scalar(T.iu[:, HALF:], T.it[:], float(HALF), None, A.add))
-    wait("V", e_im)
-    wait("V", ev(V.tensor_scalar(T.im2[:], T.im[:], 15, None, A.bitwise_and)))
-    e_mask = ev(V.tensor_scalar(T.mask[:], T.im2[:], 0.0, 4.0, A.is_equal, A.mult))
-    wait("V", e_pc)
-    e_pc4 = ev(V.tensor_scalar(T.pc4[:], T.pc[:], 0.25, None, A.mult))
-    wait("V", e_fb)
-    e_fbf = ev(V.tensor_copy(T.fbf[:], T.fbi[:]))
-    wait("g", e_fbf)
-    send([(others, T.fbl[:, me:me + 1], T.fbf[:])], "fb%d" % me)
-    wait("V", e_an)
-    e_aq = ev(V.quantize_mx(slot("aq", me), slot("asc", me), T.anb[:]))
-    wait("g", e_aq)
-    mine = slot("aq", me).bitcast(u8)
-    send([(others[:1], mine, mine)], "ac%d" % me)
-    send([(others, slot("asc", me), slot("asc", me))], "ac%d" % me)
-    send([(others[1:], mine, mine)], "ac%d" % me)
-    g.sem_inc(T.sem.vgo, 1)
-    e_i4 = ev(g.iota(T.i4[:], [[1, N]], 0, 0, allow_small_or_imprecise_dtypes=True))
-
-    order = [me] + others
-    bank = {q: T["pb" if i % 2 else "pa"] for i, q in enumerate(order)}
+    E = {}
     e_kq, e_pen, e_mm, e_v1, e_m, e_idx, e_e, e_d, e_z, e_l = [], {}, {}, {}, {}, {}, {}, {}, {}, {}
     e_h = {q: [] for q in range(N)}
+    tiles = []
 
-    def products(i):
-        q = order[i]
+    def products(q):
+        bank = T["pb" if len(tiles) % 2 else "pa"]
         if q == me:
-            wait("P", e_aq)
+            wait("P", E["aq"])
         else:
-            P.wait_ge(T.sem["ac%d" % q], 2 * count(q))
-        if i >= 2:
-            wait("P", *e_v1[order[i - 2]])
+            P.wait_ge(T.sem["ac%d" % q], 2 * count(T.cores[q]))
+        if len(tiles) >= 2:
+            wait("P", *e_v1[tiles[-2]])
+        tiles.append(q)
+        if core != home:
+            P.wait_ge(T.sem.ks, len(inner))
         e_mm[q] = []
         for b in (0, 1):
-            wait("P", e_kq[b])
+            if core == home:
+                wait("P", e_kq[b])
+            else:
+                P.wait_ge(T.sem["kc%d" % b], len(kmask[b]))
             c = slice(HALF * b, HALF * b + HALF)
-            e_mm[q].append(ev(P.matmul_mx(bank[q][:, 512 * b:512 * b + HALF], slot("aq", q), slot("asc", q),
-                                          T.kq[:, c], T.ksc[:, c], True, True)))
+            o = bank[:, 512 * b:512 * b + HALF]
+            e_mm[q].append((ev(P.matmul_mx(o, slot("aq", q), slot("asc", q), T.kq[:, c], T.ksc[:, c], True, True)), o))
         e_v1[q] = []
 
     def penalty(q):
         if q == me:
-            wait("V", e_fbf)
+            wait("V", E["fbf"])
             f = T.fbf[:]
         else:
-            V.wait_ge(T.sem["fb%d" % q], count(q))
+            V.wait_ge(T.sem["fb%d" % q], count(T.cores[q] if core == home else helper_of(q)))
             f = T.fbl[:, q:q + 1]
-        wait("V", e_iu)
+        wait("V", E["iu"])
         e_pen[q] = ev(V.tensor_scalar(T["pen%d" % q][:], T.iu[:], f, -BIG, A.is_equal, A.mult))
 
     def forbid(q, b):
-        wait("V", e_pen[q], e_mm[q][b])
+        wait("V", e_pen[q], e_mm[q][b][0])
         c = slice(HALF * b, HALF * b + HALF)
-        e_v1[q].append(ev(V.tensor_tensor(T["sp%d" % q][:, c], bank[q][:, 512 * b:512 * b + HALF], T["pen%d" % q][:, c], A.add)))
+        e_v1[q].append(ev(V.tensor_tensor(T["sp%d" % q][:, c], e_mm[q][b][1], T["pen%d" % q][:, c], A.add)))
 
     def best(q):
         wait("V", *e_v1[q])
         e_m[q] = ev(V.tensor_tensor_scan(T["m%d" % q][:, :TK], T["sp%d" % q][:], T["sp%d" % q][:], -9e29, A.max, A.max))
 
-    def spread(n, col, e_col):
-        wait("S", e_col, e_mask)
-        e_e[n] = ev(*[S.activation(T["e%d" % n][:, 32 * a:32 * a + 32], T.mask[32 * a:32 * a + 32, :], AF.Copy,
-                                   scale=col[32 * a:32 * a + 32, :]) for a in range(4)])
-
-    def first(q):
+    def index(q):
         m = T["m%d" % q]
         wait("S", e_m[q])
         e_idx[q] = ev(S.activation(T["j%d" % q][:], m[:, :TK], AF.Sign, bias=m[:, TK - 1:TK], scale=-1.0,
                                    accum_out=m[:, TK:TK + 1]))
-        spread(q, m[:, TK:TK + 1], e_idx[q])
+
+    def spread(n, qs="SSSS"):
+        col, e_col = (T.val[:], E["val"]) if n == N else (T["m%d" % n][:, TK:TK + 1], e_idx[n])
+        for qn in sorted(set(qs)):
+            wait(qn, e_col, E["mask"])
+        calls = []
+        for a in range(4):
+            o, i, s = T["e%d" % n][:, 32 * a:32 * a + 32], T.mask[32 * a:32 * a + 32, :], col[32 * a:32 * a + 32, :]
+            calls.append(S.activation(o, i, AF.Copy, scale=s) if qs[a] == "S" else V.tensor_scalar(o, i, s, None, A.mult))
+        e_e[n] = ev(*calls)
 
     def list1(n):
         wait("V", e_e[n])
         e_l[n] = ev(V.transpose(T["et%d" % n][:], T["e%d" % n][:]))
 
     def list2(n):
-        wait("V", e_l[n], e_reset)
+        wait("V", e_l[n], E["reset"])
         e_l[n] = ev(V.tensor_tensor_scan(T["ec%d" % n][:], T.reset[:], T["et%d" % n][:], 0.0, A.mult, A.add))
 
     def list3(n):
@@ -205,8 +192,101 @@ def rank_program(g, core, T, topo):
         wait("V", *e_d[n])
         e_d[n].append(ev(V.tensor_copy(T["d%d" % n][64:128, :], T["d%d" % n][0:64, :])))
 
+    def finish():
+        g.wait_ge(T.sem.loc, need["loc"])
+        waited = set(name for _, name in seen)
+        for name, n in made:
+            if name not in waited:
+                g.wait_ge(T.sem[name], n)
+
+    e_it = ev(g.iota(T.it[:], [[1, QUART]], me * TK, 0))
+    e_im = ev(g.iota(T.im[:], [[-1, 32]], 128, 1))
+    if core == home:
+        e_pc = ev(g.iota(T.pc[:], [[1, 1]], 0, 1, allow_small_or_imprecise_dtypes=True))
+        E["i4"] = ev(g.iota(T.i4[:], [[1, N]], 0, 0, allow_small_or_imprecise_dtypes=True))
+        e_an = ev(Y.dma_start(T.anb[:], T.an[:]), n=16)
+        e_fb = ev(S.dma_start(T.fbi[:], T.fb[:]), n=16)
+        e_k = [ev(S.dma_start(T.kb[:, :4 * HALF], T.k[:, :4 * HALF]), n=16),
+               ev(Y.dma_start(T.kb[:, 4 * HALF:], T.k[:, 4 * HALF:]), n=16)]
+    wait("V", e_it)
+    E["iu"] = ev(*[V.tensor_scalar(T.iu[:, b:b + QUART], T.it[:], float(b), None, A.add) for b in range(0, TK, QUART)])
+
+    def constants():
+        e_r = ev(V.memset(T.reset[:], 1.0))
+        wait("V", e_im)
+        e_i = ev(V.tensor_scalar(T.im2[:], T.im[:], 15, None, A.bitwise_and))
+        wait("V", e_r)
+        E["reset"] = ev(V.memset(T.reset[:, 0:128:16], 0.0))
+        wait("V", e_i)
+        E["mask"] = ev(V.tensor_scalar(T.mask[:], T.im2[:], 0.0, 4.0, A.is_equal, A.mult))
+
+    if core != home:
+        q = hq
+        g.wait_ge(T.sem["fb%d" % me], len(slow))
+        send([site(q, me)], T.fbl[:, me:me + 1], T.fbl[:, me:me + 1], "fb%d" % me)
+        constants()
+        penalty(q)
+        products(q)
+        forbid(q, 0)
+        forbid(q, 1)
+        best(q)
+        index(q)
+        spread(q, "SVSV")
+        wait("g", e_m[q], e_idx[q])
+        send([T.cores[q]], T.land[:, 2 * me:2 * me + 2], T["m%d" % q][:, TK - 1:TK + 1], "sc%d" % me)
+        list1(q)
+        list2(q)
+        list3(q)
+        list4(q)
+        wait("g", *e_d[q])
+        send([home], T["d%d" % q][:], T["d%d" % q][:], "dl", slow)
+        finish()
+        return
+
+    wait("V", e_fb)
+    E["fbf"] = ev(V.tensor_copy(T.fbf[:], T.fbi[:]))
+    wait("g", E["fbf"])
+    dest = [site(q, me) for q in others]
+    send([site(q, me) for q in two] + [hlp], T.fbl[:, me:me + 1], T.fbf[:], "fb%d" % me, slow)
+    wait("V", e_an)
+    E["aq"] = ev(V.quantize_mx(slot("aq", me), slot("asc", me), T.anb[:]))
+    wait("g", E["aq"])
+    mine = slot("aq", me).bitcast(u8)
+    send(dest[:1], mine, mine, "ac%d" % me)
+    send(dest, slot("asc", me), slot("asc", me), "ac%d" % me)
+    send(dest[1:], mine, mine, "ac%d" % me)
+
+    def ksend():
+        for i in (0, 1):
+            wait("V", e_k[i])
+            c = slice(HALF * i, HALF * i + HALF)
+            e_kq.append(ev(V.quantize_mx(T.kq[:, c], T.ksc[:, c], T.kb[:, 4 * HALF * i:4 * HALF * (i + 1)])))
+        for i in (0, 1):
+            c = slice(HALF * i, HALF * i + HALF)
+            wait("g", e_kq[i])
+            if i:
+                send([hlp], T.ksc[:], T.ksc[:], "ks", inner)
+            send([hlp], T.kq[:, c].bitcast(u8), T.kq[:, c].bitcast(u8), "kc%d" % i, kmask[i], "loc" if i else "lok")
+
+    def vload():
+        Y.wait_ge(T.sem.lok, need["lok"])
+        E["v"] = ev(Y.dma_start(T.vb[:], T.v[:]), n=16)
+        E["u"] = ev(Y.dma_start(T.ub[:], T.u[:]), n=16)
+
+    def own():
+        wait("Y", e_idx[me], e_m[me])
+        E["own"] = ev(Y.dma_start(T.land[:, 2 * me:2 * me + 2], T["m%d" % me][:, TK - 1:TK + 1]), n=16)
+
+    def consts2():
+        wait("V", e_pc)
+        E["pc4"] = ev(V.tensor_scalar(T.pc4[:], T.pc[:], 0.25, None, A.mult))
+
     def gather(qn, q, *ts):
-        wait(qn, e_v, *e_d[q])
+        wait(qn, E["v"])
+        if q == hq:
+            queues[qn].wait_ge(T.sem.dl, len(slow))
+        else:
+            wait(qn, *e_d[q])
         calls = []
         for t in ts:
             win, out = T.vb[:, t:4 * TK].indirect(T["d%d" % q][:, :]), T["h%d" % q][:, t:512:4]
@@ -218,103 +298,47 @@ def rank_program(g, core, T, topo):
         o, s = (slot("zq", q), slot("zsc", q)) if q == me else (T["oq%d" % q][:], T["osc%d" % q][:])
         e_z[q] = ev(V.quantize_mx(o, s, T["h%d" % q][:]))
 
-    def ship_codes(q):
+    def ship(q):
         wait("g", e_z[q])
-        send([([q], slot("zq", me).bitcast(u8), T["oq%d" % q][:].bitcast(u8))], "zc%d" % me)
+        send([T.cores[q]], slot("zq", me).bitcast(u8), T["oq%d" % q][:].bitcast(u8), "zc%d" % me)
+        send([T.cores[q]], slot("zsc", me), T["osc%d" % q][:], "zc%d" % me)
 
-    def ship_scales(*qs):
-        send([([q], slot("zsc", me), T["osc%d" % q][:]) for q in qs], "zc%d" % me)
+    def score(q):
+        wait("g", e_m[q], e_idx[q])
+        send([T.cores[q]], T.land[:, 2 * me:2 * me + 2], T["m%d" % q][:, TK - 1:TK + 1], "sc%d" % me)
 
-    r1, r2, r3 = others
-    penalty(me)
-    for i in (0, 1):
-        wait("V", e_k[i])
-        c = slice(HALF * i, HALF * i + HALF)
-        e_kq.append(ev(V.quantize_mx(T.kq[:, c], T.ksc[:, c], T.kb[:, 4 * HALF * i:4 * HALF * (i + 1)])))
-    products(0)
-    forbid(me, 0)
-    forbid(me, 1)
-    best(me)
-    first(me)
-    wait("Y", e_idx[me], e_m[me])
-    e_own = ev(Y.dma_start(T.land[:, 2 * me:2 * me + 2], T["m%d" % me][:, TK - 1:TK + 1]), n=16)
+    role = {"m": me, "a": two[0], "b": two[1], "h": hq}
+    steps = {"consts": constants, "ksend": ksend, "vload": vload, "pen": penalty, "mm": products, "f": forbid, "best": best,
+             "ix": index, "spread": spread, "own": own, "consts2": consts2, "l1": list1, "l2": list2, "l3": list3,
+             "l4": list4, "gV": lambda *x: gather("V", *x), "gS": lambda *x: gather("S", *x), "pack": pack, "ship": ship,
+             "score": score}
+    for step in PLAN.split(";"):
+        w = step.split()
+        steps[w[0]](*[role[x] if x in role else int(x) for x in w[1:]])
+
     for q in others:
-        penalty(q)
-
-    products(1)
-    forbid(r1, 0)
-    forbid(r1, 1)
-    list1(me)
-    best(r1)
-    first(r1)
-    list2(me)
-    products(2)
-    forbid(r2, 0)
-    list3(me)
-    forbid(r2, 1)
-    list4(me)
-    best(r2)
-    first(r2)
-    products(3)
-    forbid(r3, 0)
-    list1(r1)
-    forbid(r3, 1)
-    list2(r1)
-    list3(r1)
-    list4(r1)
-    gather("S", r1, 0, 1, 2, 3)
-    best(r3)
-    first(r3)
-    list1(r2)
-    list2(r2)
-    list3(r2)
-    pack(r1)
-    ship_codes(r1)
-    wait("g", *[e_m[q] for q in others] + [e_idx[q] for q in others])
-    send([([q], T.land[:, 2 * me:2 * me + 2], T["m%d" % q][:, TK - 1:TK + 1]) for q in others], "sc%d" % me)
-    list4(r2)
-    gather("V", r2, 0)
-    gather("S", r2, 2, 3)
-    list1(r3)
-    gather("V", r2, 1)
-    list2(r3)
-    list3(r3)
-    pack(r2)
-    ship_codes(r2)
-    ship_scales(r1, r2)
-    list4(r3)
-    gather("V", r3, 0, 1)
-    gather("S", r3, 2, 3)
-    pack(r3)
-    ship_codes(r3)
-    ship_scales(r3)
-
-    gather("V", me, 0, 1)
-    gather("S", me, 2, 3)
-    for q in others:
-        V.wait_ge(T.sem["sc%d" % q], count(q, (others_of(q).index(me), N - 1)))
-    wait("V", e_own)
+        V.wait_ge(T.sem["sc%d" % q], count(site(q, me)))
+    wait("V", E["own"])
     best_s = T.land[:, 0:2 * N:2]
     e_rm = ev(V.tensor_tensor_scan(T.rm[:], best_s, best_s, -9e29, A.max, A.max))
     wait("S", e_rm)
     e_qs = ev(S.activation(T.rj[:], T.rm[:], AF.Sign, bias=T.rm[:, N - 1:N], scale=-1.0, accum_out=T.qs[:]))
     pack(me)
-    wait("V", e_u)
+    wait("V", E["u"])
     e_uq = ev(V.quantize_mx(T.uq[:], T.usc[:], T.ub[:]))
-    wait("V", e_qs, e_pc4)
-    e_val = ev(V.tensor_scalar(T.val[:], T.qs[:], 32.0, T.pc4[:], A.mult, A.add))
-    spread(N, T.val, e_val)
-    wait("V", e_i4)
+    wait("V", e_qs, E["pc4"])
+    E["val"] = ev(V.tensor_scalar(T.val[:], T.qs[:], 32.0, T.pc4[:], A.mult, A.add))
+    spread(N)
+    wait("V", E["i4"])
     e_oh = ev(V.tensor_scalar(T.oh[:], T.i4[:], T.qs[:], None, A.is_equal))
 
     wait("P", e_uq)
     e_y, copies = {}, []
-    for q in order:
+    for q in [me] + two + [hq]:
         if q == me:
             wait("P", e_z[me])
         else:
-            i = others_of(q).index(me)
-            P.wait_ge(T.sem["zc%d" % q], count(q) + count(q, (i, 2) if i < 2 else None))
+            P.wait_ge(T.sem["zc%d" % q], 2 * count(T.cores[q]))
         e_y[q] = ev(P.matmul_mx(T.yp[:, 512 * q:512 * q + 128], T.uq[:], T.usc[:], slot("zq", q), slot("zsc", q), True, True))
 
     def fetch(q):
@@ -335,7 +359,7 @@ def rank_program(g, core, T, topo):
     wait("Y", e_wn)
     e_w = ev(Y.dma_start(T.win[:], T.wn[:]), n=16)
 
-    for q in others:
+    for q in two + [hq]:
         fetch(q)
     wait("V", ev(*copies))
     wait("V", *e_d[N])
@@ -343,9 +367,4 @@ def rank_program(g, core, T, topo):
     wait("Y", e_yo)
     e_out = ev(Y.dma_start(T.y[:], T.yo[:]), n=16)
     wait("Y", e_w, e_out)
-
-    g.wait_ge(T.sem.loc, need_loc[0])
-    waited = set(name for _, name in seen)
-    for name, n in made:
-        if name not in waited:
-            g.wait_ge(T.sem[name], n)
+    finish()

from concourse.bass import DstId, RemoteDMATransfer
from concourse.mybir import dt, AluOpType, AxisListType, ActivationFunctionType as AF

N, TK, HALF, QUART = 4, 640, 320, 160
BIG = 1e29
HELPED = 2

SCRATCH = {
    "anb": ("sbuf", [128, 512], "bfloat16"), "kb": ("sbuf", [128, 4 * TK], "bfloat16"),
    "vb": ("sbuf", [128, 4 * TK], "bfloat16"), "ub": ("sbuf", [128, 512], "bfloat16"),
    "aq": ("sbuf", [128, 128 * N], "float8_e4m3fn_x4"), "asc": ("sbuf", [128, 128 * N], "uint8"),
    "kq": ("sbuf", [128, TK], "float8_e4m3fn_x4"), "ksc": ("sbuf", [128, TK], "uint8"),
    "uq": ("sbuf", [128, 128], "float8_e4m3fn_x4"), "usc": ("sbuf", [128, 128], "uint8"),
    "zq": ("sbuf", [128, 128 * N], "float8_e4m3fn_x4"), "zsc": ("sbuf", [128, 128 * N], "uint8"),
    "fbi": ("sbuf", [128, 1], "int32"), "fbf": ("sbuf", [128, 1], "float32"), "fbl": ("sbuf", [128, N], "float32"),
    "it": ("sbuf", [128, QUART], "int32"), "iu": ("sbuf", [128, TK], "uint16"),
    "im": ("sbuf", [128, 32], "int32"), "im2": ("sbuf", [128, 32], "int32"), "mask": ("sbuf", [128, 32], "float32"),
    "reset": ("sbuf", [32, 128], "float32"), "pc": ("sbuf", [128, 1], "float32"), "pc4": ("sbuf", [128, 1], "float32"),
    "i4": ("sbuf", [128, N], "float32"),
    "land": ("sbuf", [128, 2 * N], "float32"), "rm": ("sbuf", [128, N], "float32"), "rj": ("sbuf", [128, N], "float32"),
    "qs": ("sbuf", [128, 1], "float32"), "val": ("sbuf", [128, 1], "float32"), "oh": ("sbuf", [128, N], "float32"),
    "ohn": ("sbuf", [128, N], "float32"), "nr": ("sbuf", [128, 1], "float32"), "wn": ("sbuf", [128, 1], "float32"),
    "yc": ("sbuf", [128, 128 * N], "float32"), "yo": ("sbuf", [128, 128], "float32"),
    "pa": ("psum", [128, 1024], "float32"), "pb": ("psum", [128, 1024], "float32"), "yp": ("psum", [128, 2048], "float32"),
}
for _q in range(N):
    SCRATCH["pen%d" % _q] = ("sbuf", [128, TK], "bfloat16")
    SCRATCH["sp%d" % _q] = ("sbuf", [128, TK], "float32")
    SCRATCH["m%d" % _q] = ("sbuf", [128, TK + 2], "float32")
    SCRATCH["j%d" % _q] = ("sbuf", [128, TK], "bfloat16")
    SCRATCH["h%d" % _q] = ("sbuf", [128, 512], "bfloat16")
    SCRATCH["oq%d" % _q] = ("sbuf", [128, 128], "float8_e4m3fn_x4")
    SCRATCH["osc%d" % _q] = ("sbuf", [128, 128], "uint8")
for _q in range(N + 1):
    SCRATCH["e%d" % _q] = ("sbuf", [32, 128], "float32")
    SCRATCH["et%d" % _q] = ("sbuf", [32, 128], "float32")
    SCRATCH["ec%d" % _q] = ("sbuf", [32, 128], "float32")
    SCRATCH["d%d" % _q] = ("sbuf", [128, 8], "uint16")

SEMAPHORES = (["x%d" % i for i in range(115)] + ["loc", "lok", "kc0", "kc1", "ks", "dl"]
              + ["fb%d" % i for i in range(N)] + ["ac%d" % i for i in range(N)] + ["sc%d" % i for i in range(N)]
              + ["zc%d" % i for i in range(N)])

PLAN = """
consts; pen m; ksend; vload; mm m; f m 0; f m 1; best m; ix m; spread m; own; consts2; pen a; pen b;
mm a; f a 0; l1 m; f a 1; l2 m; best a; ix a; spread a; score a; l3 m; mm b; f b 0; l4 m; f b 1; best b; l1 a; ix b;
spread b; score b; l2 a; l3 a; l4 a; gV a 0 1; gS a 2 3; l1 b; l2 b; l3 b; l4 b; pack a; ship a; gV b 0 1; gS b 2 3;
pack b; ship b; gV h 0 1; gS h 2 3; pack h; ship h; gV m 0 1; gS m 2 3
"""


def rank_program(g, core, T, topo):
    V, S, P, Y = g.vector, g.scalar, g.tensor, g.sync
    queues = {"g": g, "V": V, "S": S, "P": P, "Y": Y}
    u8 = dt.uint8
    A = AluOpType
    chip = [topo.chip(c) for c in T.cores]

    def others_of(r):
        near = [q for q in range(N) if q != r and topo.same_plane(chip[q], chip[r])]
        far = [q for q in range(N) if q != r and q not in near]
        far.sort(key=lambda q: (q - r) * (1 if r % 2 == 0 else -1) % N)
        return near + far

    def helper_of(r):
        c0 = T.cores[r]
        return [c for c in topo.cores_of(c0) if c != c0 and topo.die(c) == topo.die(c0)
                and all(topo.may_write(c, d) for d in T.cores)][0]

    def site(r, q):
        return helper_of(r) if q == others_of(r)[HELPED] else T.cores[r]

    owners = [r for r in range(N) if core in (T.cores[r], helper_of(r))]
    if not owners:
        return
    me, = owners
    others, home = others_of(me), T.cores[me]
    hlp, hq = helper_of(me), others_of(me)[HELPED]
    two = [q for q in others if q != hq]
    made, seen, need = [], {}, {}

    def ev(*insts, n=1):
        name = "x%d" % len(made)
        made.append((name, n * len(insts)))
        for inst in insts:
            inst.then_inc(T.sem[name], n)
        return made[-1]

    def wait(qn, *evs):
        for name, n in evs:
            if (qn, name) not in seen:
                seen[(qn, name)] = n
                queues[qn].wait_ge(T.sem[name], n)

    slow = topo.engines(home, T.cores[others[0]])
    inner = [e for e in topo.engines(home, hlp) if e not in slow]
    kmask = [inner, inner + slow]

    def count(src):
        return len(topo.engines(src, core))

    def addr(c):
        a = topo.addr(c)
        return DstId(rid=a[0], pnc=a[1])

    def send(dests, out, in_, sem, eng=None, loc="loc"):
        e = eng or topo.engines(core, dests[0])
        need[loc] = need.get(loc, 0) + len(e)
        g.remote_dma_fused([RemoteDMATransfer(dst_ids=[addr(c) for c in dests], dma_engine_mask=sum(1 << x for x in e),
                                              remote_sem=T.sem[sem], srcs=[in_], dsts=[out for _ in dests])],
                           local_sem=T.sem[loc])

    def slot(t, q):
        return T[t][:, 128 * q:128 * q + 128]

    E = {}
    e_kq, e_pen, e_mm, e_v1, e_m, e_idx, e_e, e_d, e_z, e_l = [], {}, {}, {}, {}, {}, {}, {}, {}, {}
    e_h = {q: [] for q in range(N)}
    tiles = []

    def products(q):
        bank = T["pb" if len(tiles) % 2 else "pa"]
        if q == me:
            wait("P", E["aq"])
        else:
            P.wait_ge(T.sem["ac%d" % q], 2 * count(T.cores[q]))
        if len(tiles) >= 2:
            wait("P", *e_v1[tiles[-2]])
        tiles.append(q)
        if core != home:
            P.wait_ge(T.sem.ks, len(inner))
        e_mm[q] = []
        for b in (0, 1):
            if core == home:
                wait("P", e_kq[b])
            else:
                P.wait_ge(T.sem["kc%d" % b], len(kmask[b]))
            c = slice(HALF * b, HALF * b + HALF)
            o = bank[:, 512 * b:512 * b + HALF]
            e_mm[q].append((ev(P.matmul_mx(o, slot("aq", q), slot("asc", q), T.kq[:, c], T.ksc[:, c], True, True)), o))
        e_v1[q] = []

    def penalty(q):
        if q == me:
            wait("V", E["fbf"])
            f = T.fbf[:]
        else:
            V.wait_ge(T.sem["fb%d" % q], count(T.cores[q] if core == home else helper_of(q)))
            f = T.fbl[:, q:q + 1]
        wait("V", E["iu"])
        e_pen[q] = ev(V.tensor_scalar(T["pen%d" % q][:], T.iu[:], f, -BIG, A.is_equal, A.mult))

    def forbid(q, b):
        wait("V", e_pen[q], e_mm[q][b][0])
        c = slice(HALF * b, HALF * b + HALF)
        e_v1[q].append(ev(V.tensor_tensor(T["sp%d" % q][:, c], e_mm[q][b][1], T["pen%d" % q][:, c], A.add)))

    def best(q):
        wait("V", *e_v1[q])
        e_m[q] = ev(V.tensor_tensor_scan(T["m%d" % q][:, :TK], T["sp%d" % q][:], T["sp%d" % q][:], -9e29, A.max, A.max))

    def index(q):
        m = T["m%d" % q]
        wait("S", e_m[q])
        e_idx[q] = ev(S.activation(T["j%d" % q][:], m[:, :TK], AF.Sign, bias=m[:, TK - 1:TK], scale=-1.0,
                                   accum_out=m[:, TK:TK + 1]))

    def spread(n, qs="SSSS"):
        col, e_col = (T.val[:], E["val"]) if n == N else (T["m%d" % n][:, TK:TK + 1], e_idx[n])
        for qn in sorted(set(qs)):
            wait(qn, e_col, E["mask"])
        calls = []
        for a in range(4):
            o, i, s = T["e%d" % n][:, 32 * a:32 * a + 32], T.mask[32 * a:32 * a + 32, :], col[32 * a:32 * a + 32, :]
            calls.append(S.activation(o, i, AF.Copy, scale=s) if qs[a] == "S" else V.tensor_scalar(o, i, s, None, A.mult))
        e_e[n] = ev(*calls)

    def list1(n):
        wait("V", e_e[n])
        e_l[n] = ev(V.transpose(T["et%d" % n][:], T["e%d" % n][:]))

    def list2(n):
        wait("V", e_l[n], E["reset"])
        e_l[n] = ev(V.tensor_tensor_scan(T["ec%d" % n][:], T.reset[:], T["et%d" % n][:], 0.0, A.mult, A.add))

    def list3(n):
        wait("V", e_l[n])
        d, s = T["d%d" % n], T["ec%d" % n][:, 15:128:16]
        e_d[n] = [ev(V.tensor_copy(d[0:32, :], s), V.tensor_copy(d[32:64, :], s))]

    def list4(n):
        wait("V", *e_d[n])
        e_d[n].append(ev(V.tensor_copy(T["d%d" % n][64:128, :], T["d%d" % n][0:64, :])))

    def finish():
        g.wait_ge(T.sem.loc, need["loc"])
        waited = set(name for _, name in seen)
        for name, n in made:
            if name not in waited:
                g.wait_ge(T.sem[name], n)

    e_it = ev(g.iota(T.it[:], [[1, QUART]], me * TK, 0))
    e_im = ev(g.iota(T.im[:], [[-1, 32]], 128, 1))
    if core == home:
        e_pc = ev(g.iota(T.pc[:], [[1, 1]], 0, 1, allow_small_or_imprecise_dtypes=True))
        E["i4"] = ev(g.iota(T.i4[:], [[1, N]], 0, 0, allow_small_or_imprecise_dtypes=True))
        e_an = ev(Y.dma_start(T.anb[:], T.an[:]), n=16)
        e_fb = ev(S.dma_start(T.fbi[:], T.fb[:]), n=16)
        e_k = [ev(S.dma_start(T.kb[:, :4 * HALF], T.k[:, :4 * HALF]), n=16),
               ev(Y.dma_start(T.kb[:, 4 * HALF:], T.k[:, 4 * HALF:]), n=16)]
    wait("V", e_it)
    E["iu"] = ev(*[V.tensor_scalar(T.iu[:, b:b + QUART], T.it[:], float(b), None, A.add) for b in range(0, TK, QUART)])

    def constants():
        e_r = ev(V.memset(T.reset[:], 1.0))
        wait("V", e_im)
        e_i = ev(V.tensor_scalar(T.im2[:], T.im[:], 15, None, A.bitwise_and))
        wait("V", e_r)
        E["reset"] = ev(V.memset(T.reset[:, 0:128:16], 0.0))
        wait("V", e_i)
        E["mask"] = ev(V.tensor_scalar(T.mask[:], T.im2[:], 0.0, 4.0, A.is_equal, A.mult))

    if core != home:
        q = hq
        g.wait_ge(T.sem["fb%d" % me], len(slow))
        send([site(q, me)], T.fbl[:, me:me + 1], T.fbl[:, me:me + 1], "fb%d" % me)
        constants()
        penalty(q)
        products(q)
        forbid(q, 0)
        forbid(q, 1)
        best(q)
        index(q)
        spread(q, "SVSV")
        wait("g", e_m[q], e_idx[q])
        send([T.cores[q]], T.land[:, 2 * me:2 * me + 2], T["m%d" % q][:, TK - 1:TK + 1], "sc%d" % me)
        list1(q)
        list2(q)
        list3(q)
        list4(q)
        wait("g", *e_d[q])
        send([home], T["d%d" % q][:], T["d%d" % q][:], "dl", slow)
        finish()
        return

    wait("V", e_fb)
    E["fbf"] = ev(V.tensor_copy(T.fbf[:], T.fbi[:]))
    wait("g", E["fbf"])
    dest = [site(q, me) for q in others]
    send([site(q, me) for q in two] + [hlp], T.fbl[:, me:me + 1], T.fbf[:], "fb%d" % me, slow)
    wait("V", e_an)
    E["aq"] = ev(V.quantize_mx(slot("aq", me), slot("asc", me), T.anb[:]))
    wait("g", E["aq"])
    mine = slot("aq", me).bitcast(u8)
    send(dest[:1], mine, mine, "ac%d" % me)
    send(dest, slot("asc", me), slot("asc", me), "ac%d" % me)
    send(dest[1:], mine, mine, "ac%d" % me)

    def ksend():
        for i in (0, 1):
            wait("V", e_k[i])
            c = slice(HALF * i, HALF * i + HALF)
            e_kq.append(ev(V.quantize_mx(T.kq[:, c], T.ksc[:, c], T.kb[:, 4 * HALF * i:4 * HALF * (i + 1)])))
        for i in (0, 1):
            c = slice(HALF * i, HALF * i + HALF)
            wait("g", e_kq[i])
            if i:
                send([hlp], T.ksc[:], T.ksc[:], "ks", inner)
            send([hlp], T.kq[:, c].bitcast(u8), T.kq[:, c].bitcast(u8), "kc%d" % i, kmask[i], "loc" if i else "lok")

    def vload():
        Y.wait_ge(T.sem.lok, need["lok"])
        E["v"] = ev(Y.dma_start(T.vb[:], T.v[:]), n=16)
        E["u"] = ev(Y.dma_start(T.ub[:], T.u[:]), n=16)

    def own():
        wait("Y", e_idx[me], e_m[me])
        E["own"] = ev(Y.dma_start(T.land[:, 2 * me:2 * me + 2], T["m%d" % me][:, TK - 1:TK + 1]), n=16)

    def consts2():
        wait("V", e_pc)
        E["pc4"] = ev(V.tensor_scalar(T.pc4[:], T.pc[:], 0.25, None, A.mult))

    def gather(qn, q, *ts):
        wait(qn, E["v"])
        if q == hq:
            queues[qn].wait_ge(T.sem.dl, len(slow))
        else:
            wait(qn, *e_d[q])
        calls = []
        for t in ts:
            win, out = T.vb[:, t:4 * TK].indirect(T["d%d" % q][:, :]), T["h%d" % q][:, t:512:4]
            calls.append(V.tensor_copy(out, win) if qn == "V" else S.activation(out, win, AF.Copy))
        e_h[q].append(ev(*calls))

    def pack(q):
        wait("V", *e_h[q])
        o, s = (slot("zq", q), slot("zsc", q)) if q == me else (T["oq%d" % q][:], T["osc%d" % q][:])
        e_z[q] = ev(V.quantize_mx(o, s, T["h%d" % q][:]))

    def ship(q):
        wait("g", e_z[q])
        send([T.cores[q]], slot("zq", me).bitcast(u8), T["oq%d" % q][:].bitcast(u8), "zc%d" % me)
        send([T.cores[q]], slot("zsc", me), T["osc%d" % q][:], "zc%d" % me)

    def score(q):
        wait("g", e_m[q], e_idx[q])
        send([T.cores[q]], T.land[:, 2 * me:2 * me + 2], T["m%d" % q][:, TK - 1:TK + 1], "sc%d" % me)

    role = {"m": me, "a": two[0], "b": two[1], "h": hq}
    steps = {"consts": constants, "ksend": ksend, "vload": vload, "pen": penalty, "mm": products, "f": forbid, "best": best,
             "ix": index, "spread": spread, "own": own, "consts2": consts2, "l1": list1, "l2": list2, "l3": list3,
             "l4": list4, "gV": lambda *x: gather("V", *x), "gS": lambda *x: gather("S", *x), "pack": pack, "ship": ship,
             "score": score}
    for step in PLAN.split(";"):
        w = step.split()
        steps[w[0]](*[role[x] if x in role else int(x) for x in w[1:]])

    for q in others:
        V.wait_ge(T.sem["sc%d" % q], count(site(q, me)))
    wait("V", E["own"])
    best_s = T.land[:, 0:2 * N:2]
    e_rm = ev(V.tensor_tensor_scan(T.rm[:], best_s, best_s, -9e29, A.max, A.max))
    wait("S", e_rm)
    e_qs = ev(S.activation(T.rj[:], T.rm[:], AF.Sign, bias=T.rm[:, N - 1:N], scale=-1.0, accum_out=T.qs[:]))
    pack(me)
    wait("V", E["u"])
    e_uq = ev(V.quantize_mx(T.uq[:], T.usc[:], T.ub[:]))
    wait("V", e_qs, E["pc4"])
    E["val"] = ev(V.tensor_scalar(T.val[:], T.qs[:], 32.0, T.pc4[:], A.mult, A.add))
    spread(N)
    wait("V", E["i4"])
    e_oh = ev(V.tensor_scalar(T.oh[:], T.i4[:], T.qs[:], None, A.is_equal))

    wait("P", e_uq)
    e_y, copies = {}, []
    for q in [me] + two + [hq]:
        if q == me:
            wait("P", e_z[me])
        else:
            P.wait_ge(T.sem["zc%d" % q], 2 * count(T.cores[q]))
        e_y[q] = ev(P.matmul_mx(T.yp[:, 512 * q:512 * q + 128], T.uq[:], T.usc[:], slot("zq", q), slot("zsc", q), True, True))

    def fetch(q):
        wait("V", e_y[q])
        copies.append(V.tensor_copy(slot("yc", q), T.yp[:, 512 * q:512 * q + 128]))

    fetch(me)
    list1(N)
    wait("V", e_oh)
    e_ohn = ev(V.tensor_tensor(T.ohn[:], T.oh[:], T.land[:, 1:2 * N:2], A.mult))
    list2(N)
    wait("V", e_ohn)
    e_nr = ev(V.tensor_reduce(T.nr[:], T.ohn[:], AxisListType.X, A.add))
    list3(N)
    wait("V", e_nr)
    e_wn = ev(V.tensor_scalar(T.wn[:], T.qs[:], float(TK), T.nr[:], A.mult, A.add))
    list4(N)
    wait("Y", e_wn)
    e_w = ev(Y.dma_start(T.win[:], T.wn[:]), n=16)

    for q in two + [hq]:
        fetch(q)
    wait("V", ev(*copies))
    wait("V", *e_d[N])
    e_yo = ev(V.tensor_copy(T.yo[:], T.yc[:].indirect(T["d%d" % N][:, :])))
    wait("Y", e_yo)
    e_out = ev(Y.dma_start(T.y[:], T.yo[:]), n=16)
    wait("Y", e_w, e_out)
    finish()
